import numpy as np
import ml_dtypes


def mxq(x, axis, fmt="e4m3"):
    dtype, down = {"e4m3": (ml_dtypes.float8_e4m3fn, 7), "e5m2": (ml_dtypes.float8_e5m2, 14)}[fmt]
    v = np.moveaxis(np.asarray(x, np.float32).astype(ml_dtypes.bfloat16).astype(np.float64), axis, -1)
    blocks = v.reshape(v.shape[:-1] + (-1, 32))
    amax = np.abs(blocks).max(-1, keepdims=True)
    byte = np.maximum(np.where(amax > 0, np.frexp(amax)[1] - 1 + 127, 0) - down, 1)
    scale = np.exp2(byte - 127.0)
    codes = (blocks / scale).astype(np.float32).astype(dtype).astype(np.float64)
    return np.moveaxis((codes * scale).reshape(v.shape), -1, axis)


WIDE = False


def mx_kscale(k):
    if not WIDE:
        return np.ones(k)
    levels = np.array([10, -10, 5, -5, 0])
    if k % 512:
        return np.exp2(np.random.permutation(np.resize(levels, k // 32))).repeat(32)
    a = np.empty((k // 512, 16))
    for p in range(k // 512):
        a[p, :8] = np.random.permutation(np.resize(levels, 8))
        for g in range(8):
            far = levels[np.abs(levels - a[p, g]) >= 10]
            a[p, g + 8] = far[np.random.randint(len(far))]
    return np.exp2(a.ravel()).repeat(32)


def f64(x):
    return np.asarray(x).astype(np.float64)


def striped(idx):
    return np.tile(np.asarray(idx).reshape(-1, 16).T, (8, 1)).astype(np.uint16)


def unstriped(offs):
    return offs[:16].T.reshape(-1).astype(np.int64)


D, T, U, I, G, M = 512, 1024, 1024, 512, 64, 128


def setup_inputs():
    n = np.random.standard_normal
    idx = np.repeat(np.random.permutation(T)[:G], I // G)
    idx2 = np.random.permutation(U)[:I]
    fd = mx_kscale(D)
    return {
        "fa": (n((D, T)) / fd[:, None]).astype(np.float32),
        "fb": (n((D, U))).astype(np.float32),
        "wg": (n((D, M)) * 1 / np.sqrt(D) * fd[:, None]).astype(np.float32),
        "disp": (np.random.uniform(0.0, 8.0, (1, I))).astype(np.float32),
        "offs": striped(idx),
        "offs2": striped(idx2),
    }


def reference(fa, fb, wg, disp, offs, offs2):
    idx = unstriped(offs)
    idx2 = unstriped(offs2)
    x = f64(fa)[:, idx] * f64(fb)[:, idx2]
    wgq = mxq(f64(wg), 0, "e4m3")
    xq = mxq(x, 0, "e4m3")
    a = wgq.T @ xq
    p = np.exp(a)
    s = p.reshape(M, G, I // G).sum(axis=2)
    y = (p * f64(disp)).reshape(M, G, I // G).sum(axis=2) / s
    return y

@@ -1,0 +1,159 @@
+from contextlib import ExitStack
+
+import concourse.mybir as mybir
+from concourse.masks import make_identity
+
+F32 = mybir.dt.float32
+BF16 = mybir.dt.bfloat16
+U32 = mybir.dt.uint32
+U16 = mybir.dt.uint16
+U8 = mybir.dt.uint8
+FP8X4 = mybir.dt.float8_e4m3fn_x4
+ALU = mybir.AluOpType
+ACT = mybir.ActivationFunctionType
+AX = mybir.AxisListType
+
+P = 128
+PACK = 4
+D, T, I, G, M = 512, 1024, 512, 64, 128
+J = I // G
+CHUNKS = 4
+CI = I // CHUNKS
+CG = G // CHUNKS
+CL = CI // 16
+
+FLOPS = 2 * D * M * I
+
+
+def tile_attend_costvolume_kernel(tc, fa, fb, wg, disp, offs, offs2, out):
+    nc = tc.nc
+    with ExitStack() as ctx:
+        sb = ctx.enter_context(tc.tile_pool(name="sb", bufs=1))
+        ps = ctx.enter_context(tc.psum_pool(name="ps", bufs=1))
+
+        list_a = sb.tile([P, I // 16], U16, name="list_a")
+        list_b = sb.tile([P, I // 16], U16, name="list_b")
+        a_planes = [sb.tile([P, T], F32, name="a%d" % t) for t in range(PACK)]
+        b_planes = [sb.tile([P, T], F32, name="b%d" % t) for t in range(PACK)]
+        w_raw = sb.tile([P, PACK, M], F32, name="w_raw")
+        d_cols = sb.tile([P, PACK], F32, name="d_cols")
+        fa_v = fa.rearrange("(p t) c -> p t c", t=PACK)
+        fb_v = fb.rearrange("(p t) c -> p t c", t=PACK)
+
+        nc.sync.dma_start(list_b[:], offs2)
+        nc.sync.dma_start(b_planes[0][:], fb_v[:, 0, :])
+        nc.sync.dma_start(list_a[:], offs)
+        nc.sync.dma_start(a_planes[0][:], fa_v[:, 0, :])
+        nc.sync.dma_start(d_cols[:], disp.rearrange("o (n q) -> (o n) q", q=PACK))
+        nc.sync.dma_start(w_raw[:], wg.rearrange("(p t) m -> p t m", t=PACK))
+        nc.sync.dma_start(b_planes[1][:], fb_v[:, 1, :])
+        nc.sync.dma_start(a_planes[1][:], fa_v[:, 1, :])
+        nc.sync.dma_start(b_planes[2][:], fb_v[:, 2, :])
+        nc.sync.dma_start(b_planes[3][:], fb_v[:, 3, :])
+        nc.sync.dma_start(a_planes[2][:], fa_v[:, 2, :])
+        nc.sync.dma_start(a_planes[3][:], fa_v[:, 3, :])
+
+        warm = sb.tile([P, 1], F32, name="warm")
+        warm_out = sb.tile([P, 1], F32, name="warm_out")
+        nc.vector.memset(warm[:], 0.0)
+        nc.scalar.activation(warm_out[:], warm[:], ACT.Exp)
+
+        ident = sb.tile([P, P], F32, name="ident")
+        make_identity(nc, ident[:])
+
+        b_got = [sb.tile([P, I], F32, name="bg%d" % t) for t in range(PACK)]
+        x01 = sb.tile([P, 2, I], F32, name="x01")
+        x23 = [sb.tile([P, 2, CI], F32, name="x23_%d" % c) for c in range(CHUNKS)]
+        xw = [sb.tile([P, CI, PACK], BF16, name="xw%d" % c, align_bytes=64) for c in range(CHUNKS)]
+
+        def gather_b(t):
+            nc.vector.tensor_copy(b_got[t][:], b_planes[t][:].indirect(list_b[:]))
+
+        def cols(c):
+            return slice(c * CI, (c + 1) * CI)
+
+        def product_chunk(t, c):
+            nc.vector.tensor_tensor(
+                x23[c][:, t - 2, :],
+                a_planes[t][:].indirect(list_a[:, c * CL : (c + 1) * CL]),
+                b_got[t][:, cols(c)],
+                ALU.mult,
+            )
+
+        gather_b(0)
+        nc.vector.tensor_tensor(x01[:, 0, :], a_planes[0][:].indirect(list_a[:]), b_got[0][:], ALU.mult)
+
+        d_ps = ps.tile([P, PACK, P], F32, name="d_ps")
+        for q in range(PACK):
+            nc.tensor.transpose(d_ps[:, q, :], d_cols[:, q : q + 1].to_broadcast([P, P]), ident[:])
+        d_all = sb.tile([P, P, PACK], F32, name="d_all")
+        nc.scalar.copy(d_all[:], d_ps[:].rearrange("p q n -> p n q"))
+        d_flat = d_all[:].rearrange("p n q -> p (n q)")
+
+        ww = sb.tile([P, M, PACK], BF16, name="ww", align_bytes=64)
+        nc.scalar.copy(ww[:], w_raw[:].rearrange("p t m -> p m t"))
+        w_codes = sb.tile([P, M], U32, name="w_codes", align_bytes=64)
+        w_scales = sb.tile([P, M], U8, name="w_scales", align_bytes=64)
+        nc.vector.quantize_mx(out=w_codes[:].bitcast(FP8X4), scales=w_scales[:], in_=ww[:].rearrange("p m t -> p (m t)"))
+
+        gather_b(1)
+        nc.vector.tensor_tensor(x01[:, 1, :], a_planes[1][:].indirect(list_a[:]), b_got[1][:], ALU.mult)
+        for c in range(CHUNKS):
+            nc.scalar.copy(xw[c][:, :, 0:2], x01[:, :, cols(c)].rearrange("p t i -> p i t"))
+        gather_b(2)
+        gather_b(3)
+        for c in range(CHUNKS):
+            product_chunk(2, c)
+        for c in range(CHUNKS):
+            product_chunk(3, c)
+            nc.scalar.copy(xw[c][:, :, 2:4], x23[c][:].rearrange("p t i -> p i t"))
+
+        acc = [ps.tile([M, CG, J], F32, name="acc%d" % c) for c in range(CHUNKS)]
+        top = [sb.tile([P, CG], F32, name="top%d" % c) for c in range(CHUNKS)]
+        z = [sb.tile([P, CG, J], F32, name="z%d" % c) for c in range(CHUNKS)]
+        pr = [sb.tile([P, CG, J], F32, name="pr%d" % c) for c in range(CHUNKS)]
+        pd = [sb.tile([P, CG, J], F32, name="pd%d" % c) for c in range(CHUNKS)]
+        den = [sb.tile([P, CG], F32, name="den%d" % c) for c in range(CHUNKS)]
+        num = [sb.tile([P, CG], F32, name="num%d" % c) for c in range(CHUNKS)]
+        inv = [sb.tile([P, CG], F32, name="inv%d" % c) for c in range(CHUNKS)]
+        res = sb.tile([P, G], F32, name="res")
+
+        def scores(c):
+            codes = sb.tile([P, CI], U32, name="xc%d" % c, align_bytes=64)
+            scales = sb.tile([P, CI], U8, name="xs%d" % c, align_bytes=64)
+            nc.vector.quantize_mx(out=codes[:].bitcast(FP8X4), scales=scales[:], in_=xw[c][:].rearrange("p i t -> p (i t)"))
+            nc.tensor.matmul_mx(
+                out=acc[c][:].rearrange("p g j -> p (g j)"),
+                lhsT=w_codes[:].bitcast(FP8X4),
+                lhsT_scale=w_scales[:],
+                rhs=codes[:].bitcast(FP8X4),
+                rhs_scale=scales[:],
+                start=True,
+                stop=True,
+            )
+
+        def largest(c):
+            nc.vector.tensor_reduce(top[c][:], acc[c][:], AX.X, ALU.max)
+
+        def shift(c):
+            nc.vector.tensor_tensor(z[c][:], acc[c][:], top[c][:].unsqueeze(2).to_broadcast([P, CG, J]), ALU.subtract)
+            nc.scalar.activation(pr[c][:], z[c][:], ACT.Exp)
+
+        def weigh(c):
+            nc.vector.tensor_reduce(den[c][:], pr[c][:], AX.X, ALU.add)
+            nc.vector.tensor_tensor(pd[c][:].rearrange("p g j -> p (g j)"), pr[c][:].rearrange("p g j -> p (g j)"), d_flat[:, cols(c)], ALU.mult)
+
+        def sums(c):
+            nc.vector.reciprocal(inv[c][:], den[c][:])
+            nc.vector.tensor_reduce(num[c][:], pd[c][:], AX.X, ALU.add)
+
+        def finish(c):
+            nc.vector.tensor_tensor(res[:, c * CG : (c + 1) * CG], num[c][:], inv[c][:], ALU.mult)
+
+        stages = [scores, largest, shift, weigh, sums, finish]
+        for step in range(CHUNKS + len(stages) - 1):
+            for s in range(len(stages)):
+                c = step - s
+                if 0 <= c < CHUNKS:
+                    stages[s](c)
+        nc.sync.dma_start(out, res[:])

@@ -40,11 +40,11 @@ def tile_attend_costvolume_kernel(tc, fa, fb, wg, disp, offs, offs2, out):
         fa_v = fa.rearrange("(p t) c -> p t c", t=PACK)
         fb_v = fb.rearrange("(p t) c -> p t c", t=PACK)
 
-        nc.sync.dma_start(list_b[:], offs2)
         nc.sync.dma_start(b_planes[0][:], fb_v[:, 0, :])
+        nc.sync.dma_start(list_b[:], offs2)
         nc.sync.dma_start(list_a[:], offs)
         nc.sync.dma_start(a_planes[0][:], fa_v[:, 0, :])
-        nc.sync.dma_start(d_cols[:], disp.rearrange("o (n q) -> (o n) q", q=PACK))
+        nc.scalar.dma_start(d_cols[:], disp.rearrange("o (n q) -> (o n) q", q=PACK))
         nc.sync.dma_start(w_raw[:], wg.rearrange("(p t) m -> p t m", t=PACK))
         nc.sync.dma_start(b_planes[1][:], fb_v[:, 1, :])
         nc.sync.dma_start(a_planes[1][:], fa_v[:, 1, :])
@@ -106,7 +106,10 @@ def tile_attend_costvolume_kernel(tc, fa, fb, wg, disp, offs, offs2, out):
             product_chunk(2, c)
         for c in range(CHUNKS):
             product_chunk(3, c)
-            nc.scalar.copy(xw[c][:, :, 2:4], x23[c][:].rearrange("p t i -> p i t"))
+            if c % 2 == 0:
+                nc.vector.tensor_copy(xw[c][:, :, 2:4], x23[c][:].rearrange("p t i -> p i t"))
+            else:
+                nc.scalar.copy(xw[c][:, :, 2:4], x23[c][:].rearrange("p t i -> p i t"))
 
         acc = [ps.tile([M, CG, J], F32, name="acc%d" % c) for c in range(CHUNKS)]
         top = [sb.tile([P, CG], F32, name="top%d" % c) for c in range(CHUNKS)]
@@ -114,8 +117,8 @@ def tile_attend_costvolume_kernel(tc, fa, fb, wg, disp, offs, offs2, out):
         pr = [sb.tile([P, CG, J], F32, name="pr%d" % c) for c in range(CHUNKS)]
         pd = [sb.tile([P, CG, J], F32, name="pd%d" % c) for c in range(CHUNKS)]
         den = [sb.tile([P, CG], F32, name="den%d" % c) for c in range(CHUNKS)]
-        num = [sb.tile([P, CG], F32, name="num%d" % c) for c in range(CHUNKS)]
-        inv = [sb.tile([P, CG], F32, name="inv%d" % c) for c in range(CHUNKS)]
+        num = sb.tile([P, G], F32, name="num")
+        inv = sb.tile([P, G], F32, name="inv")
         res = sb.tile([P, G], F32, name="res")
 
         def scores(c):
@@ -141,19 +144,28 @@ def tile_attend_costvolume_kernel(tc, fa, fb, wg, disp, offs, offs2, out):
 
         def weigh(c):
             nc.vector.tensor_reduce(den[c][:], pr[c][:], AX.X, ALU.add)
-            nc.vector.tensor_tensor(pd[c][:].rearrange("p g j -> p (g j)"), pr[c][:].rearrange("p g j -> p (g j)"), d_flat[:, cols(c)], ALU.mult)
+            eng = nc.vector if c == CHUNKS - 1 else nc.gpsimd
+            eng.tensor_tensor(pd[c][:].rearrange("p g j -> p (g j)"), pr[c][:].rearrange("p g j -> p (g j)"), d_flat[:, cols(c)], ALU.mult)
 
         def sums(c):
-            nc.vector.reciprocal(inv[c][:], den[c][:])
-            nc.vector.tensor_reduce(num[c][:], pd[c][:], AX.X, ALU.add)
+            nc.vector.reciprocal(inv[:, c * CG : (c + 1) * CG], den[c][:])
+            nc.vector.tensor_reduce(num[:, c * CG : (c + 1) * CG], pd[c][:], AX.X, ALU.add)
 
-        def finish(c):
-            nc.vector.tensor_tensor(res[:, c * CG : (c + 1) * CG], num[c][:], inv[c][:], ALU.mult)
+        def finish(first, last):
+            span = slice(first * CG, (last + 1) * CG)
+            nc.vector.tensor_tensor(res[:, span], num[:, span], inv[:, span], ALU.mult)
 
-        stages = [scores, largest, shift, weigh, sums, finish]
-        for step in range(CHUNKS + len(stages) - 1):
-            for s in range(len(stages)):
-                c = step - s
-                if 0 <= c < CHUNKS:
-                    stages[s](c)
+        for c in range(CHUNKS):
+            scores(c)
+        for c in range(CHUNKS):
+            largest(c)
+            shift(c)
+        last = CHUNKS - 1
+        weigh(last)
+        sums(last)
+        for c in range(last):
+            weigh(c)
+        for c in range(last):
+            sums(c)
+        finish(0, last)
         nc.sync.dma_start(out, res[:])

@@ -17,12 +17,24 @@ P = 128
 PACK = 4
 D, T, I, G, M = 512, 1024, 512, 64, 128
 J = I // G
-CHUNKS = 4
-CI = I // CHUNKS
-CG = G // CHUNKS
-CL = CI // 16
+PRODUCTS = [64, 128, 128, 64, 128]
+WEAVES = [(64, "s"), (128, "v"), (128, "v"), (64, "s"), (128, "s")]
+PASSES = [64, 128, 128, 64, 128]
+BANKS = [64, 128, 128, 64, 128]
 
 FLOPS = 2 * D * M * I
+
+
+def spans(widths):
+    out, at = [], 0
+    for w in widths:
+        out.append((at, at + w))
+        at = at + w
+    return out
+
+
+def holder(ranges, lo):
+    return [k for k, (a, b) in enumerate(ranges) if a <= lo < b][0]
 
 
 def tile_attend_costvolume_kernel(tc, fa, fb, wg, disp, offs, offs2, out):
@@ -37,6 +49,7 @@ def tile_attend_costvolume_kernel(tc, fa, fb, wg, disp, offs, offs2, out):
         b_planes = [sb.tile([P, T], F32, name="b%d" % t) for t in range(PACK)]
         w_raw = sb.tile([P, PACK, M], F32, name="w_raw")
         d_cols = sb.tile([P, PACK], F32, name="d_cols")
+        d_rows = sb.tile([P, P], F32, name="d_rows")
         fa_v = fa.rearrange("(p t) c -> p t c", t=PACK)
         fb_v = fb.rearrange("(p t) c -> p t c", t=PACK)
 
@@ -44,89 +57,109 @@ def tile_attend_costvolume_kernel(tc, fa, fb, wg, disp, offs, offs2, out):
         nc.sync.dma_start(list_b[:], offs2)
         nc.sync.dma_start(list_a[:], offs)
         nc.sync.dma_start(a_planes[0][:], fa_v[:, 0, :])
-        nc.scalar.dma_start(d_cols[:], disp.rearrange("o (n q) -> (o n) q", q=PACK))
-        nc.sync.dma_start(w_raw[:], wg.rearrange("(p t) m -> p t m", t=PACK))
+        nc.gpsimd.memset(d_rows[:], 0.0)
+        nc.scalar.dma_start(d_rows[0:PACK, :], disp.rearrange("o (q n) -> (o q) n", q=PACK))
         nc.sync.dma_start(b_planes[1][:], fb_v[:, 1, :])
         nc.sync.dma_start(a_planes[1][:], fa_v[:, 1, :])
         nc.sync.dma_start(b_planes[2][:], fb_v[:, 2, :])
         nc.sync.dma_start(b_planes[3][:], fb_v[:, 3, :])
         nc.sync.dma_start(a_planes[2][:], fa_v[:, 2, :])
         nc.sync.dma_start(a_planes[3][:], fa_v[:, 3, :])
-
-        warm = sb.tile([P, 1], F32, name="warm")
-        warm_out = sb.tile([P, 1], F32, name="warm_out")
-        nc.vector.memset(warm[:], 0.0)
-        nc.scalar.activation(warm_out[:], warm[:], ACT.Exp)
+        nc.sync.dma_start(w_raw[:], wg.rearrange("(p t) m -> p t m", t=PACK))
 
         ident = sb.tile([P, P], F32, name="ident")
         make_identity(nc, ident[:])
 
-        b_got = [sb.tile([P, I], F32, name="bg%d" % t) for t in range(PACK)]
+        prods = spans(PRODUCTS)
+        weaves = spans([w for w, e in WEAVES])
+        passes = spans(PASSES)
+        banks = spans(BANKS)
+        b_got = [sb.tile([P, I], F32, name="bg%d" % t) for t in range(PACK - 1)]
+        HEAD = 192
+        b3_head = sb.tile([P, HEAD], F32, name="b3_head", tag="head", align_bytes=64)
+        b3_rest = sb.tile([P, I - HEAD], F32, name="b3_rest")
         x01 = sb.tile([P, 2, I], F32, name="x01")
-        x23 = [sb.tile([P, 2, CI], F32, name="x23_%d" % c) for c in range(CHUNKS)]
-        xw = [sb.tile([P, CI, PACK], BF16, name="xw%d" % c, align_bytes=64) for c in range(CHUNKS)]
+        x23 = [sb.tile([P, 2, b - a], F32, name="x23_%d" % c) for c, (a, b) in enumerate(prods)]
+        xw = [sb.tile([P, b - a, PACK], BF16, name="xw%d" % c, align_bytes=64) for c, (a, b) in enumerate(passes)]
 
         def gather_b(t):
             nc.vector.tensor_copy(b_got[t][:], b_planes[t][:].indirect(list_b[:]))
 
-        def cols(c):
-            return slice(c * CI, (c + 1) * CI)
-
-        def product_chunk(t, c):
+        def product(t, c):
+            a, b = prods[c]
             nc.vector.tensor_tensor(
                 x23[c][:, t - 2, :],
-                a_planes[t][:].indirect(list_a[:, c * CL : (c + 1) * CL]),
-                b_got[t][:, cols(c)],
+                a_planes[t][:].indirect(list_a[:, a // 16 : b // 16]),
+                b_got[t][:, a:b] if t < 3 else (b3_head[:, a:b] if b <= HEAD else b3_rest[:, a - HEAD : b - HEAD]),
                 ALU.mult,
             )
+
+        def weave(k):
+            a, b = weaves[k]
+            c, q = holder(prods, a), holder(passes, a)
+            dst = xw[q][:, a - passes[q][0] : b - passes[q][0], 2:4]
+            src = x23[c][:, :, a - prods[c][0] : b - prods[c][0]].rearrange("p t i -> p i t")
+            if WEAVES[k][1] == "v":
+                nc.vector.tensor_copy(dst, src)
+            else:
+                nc.scalar.copy(dst, src)
 
         gather_b(0)
         nc.vector.tensor_tensor(x01[:, 0, :], a_planes[0][:].indirect(list_a[:]), b_got[0][:], ALU.mult)
 
+        d_turned = ps.tile([P, P], F32, name="d_turned")
+        nc.tensor.transpose(d_turned[:], d_rows[:], ident[:])
+        nc.scalar.copy(d_cols[:], d_turned[:, 0:PACK])
         d_ps = ps.tile([P, PACK, P], F32, name="d_ps")
         for q in range(PACK):
             nc.tensor.transpose(d_ps[:, q, :], d_cols[:, q : q + 1].to_broadcast([P, P]), ident[:])
-        d_all = sb.tile([P, P, PACK], F32, name="d_all")
-        nc.scalar.copy(d_all[:], d_ps[:].rearrange("p q n -> p n q"))
-        d_flat = d_all[:].rearrange("p n q -> p (n q)")
+        d_all = sb.tile([P, PACK, P], F32, name="d_all")
+        nc.scalar.copy(d_all[:], d_ps[:])
+        d_flat = d_all[:].rearrange("p q n -> p (q n)")
 
-        ww = sb.tile([P, M, PACK], BF16, name="ww", align_bytes=64)
-        nc.scalar.copy(ww[:], w_raw[:].rearrange("p t m -> p m t"))
         w_codes = sb.tile([P, M], U32, name="w_codes", align_bytes=64)
         w_scales = sb.tile([P, M], U8, name="w_scales", align_bytes=64)
-        nc.vector.quantize_mx(out=w_codes[:].bitcast(FP8X4), scales=w_scales[:], in_=ww[:].rearrange("p m t -> p (m t)"))
+
+        def weights():
+            ww = sb.tile([P, M, PACK], BF16, name="ww", tag="head", align_bytes=64)
+            nc.scalar.copy(ww[:, 0:96, :], w_raw[:, :, 0:96].rearrange("p t m -> p m t"))
+            return ww
+
+        def weights_rest(ww):
+            nc.vector.tensor_copy(ww[:, 96:M, :], w_raw[:, :, 96:M].rearrange("p t m -> p m t"))
+            nc.vector.quantize_mx(out=w_codes[:].bitcast(FP8X4), scales=w_scales[:], in_=ww[:].rearrange("p m t -> p (m t)"))
 
         gather_b(1)
         nc.vector.tensor_tensor(x01[:, 1, :], a_planes[1][:].indirect(list_a[:]), b_got[1][:], ALU.mult)
-        for c in range(CHUNKS):
-            nc.scalar.copy(xw[c][:, :, 0:2], x01[:, :, cols(c)].rearrange("p t i -> p i t"))
+        for q, (a, b) in enumerate(passes):
+            nc.scalar.copy(xw[q][:, :, 0:2], x01[:, :, a:b].rearrange("p t i -> p i t"))
         gather_b(2)
-        gather_b(3)
-        for c in range(CHUNKS):
-            product_chunk(2, c)
-        for c in range(CHUNKS):
-            product_chunk(3, c)
-            if c % 2 == 0:
-                nc.vector.tensor_copy(xw[c][:, :, 2:4], x23[c][:].rearrange("p t i -> p i t"))
-            else:
-                nc.scalar.copy(xw[c][:, :, 2:4], x23[c][:].rearrange("p t i -> p i t"))
+        nc.vector.tensor_copy(b3_head[:], b_planes[3][:].indirect(list_b[:, 0 : HEAD // 16]))
+        nc.vector.tensor_copy(b3_rest[:], b_planes[3][:].indirect(list_b[:, HEAD // 16 : I // 16]))
+        for c in range(len(prods)):
+            product(2, c)
 
-        acc = [ps.tile([M, CG, J], F32, name="acc%d" % c) for c in range(CHUNKS)]
-        top = [sb.tile([P, CG], F32, name="top%d" % c) for c in range(CHUNKS)]
-        z = [sb.tile([P, CG, J], F32, name="z%d" % c) for c in range(CHUNKS)]
-        pr = [sb.tile([P, CG, J], F32, name="pr%d" % c) for c in range(CHUNKS)]
-        pd = [sb.tile([P, CG, J], F32, name="pd%d" % c) for c in range(CHUNKS)]
-        den = [sb.tile([P, CG], F32, name="den%d" % c) for c in range(CHUNKS)]
+        acc = [ps.tile([M, b - a], F32, name="acc%d" % c) for c, (a, b) in enumerate(banks)]
+        top = sb.tile([P, G], F32, name="top")
+        z = sb.tile([P, I], F32, name="z")
+        pr = sb.tile([P, I], F32, name="pr")
+        pd = sb.tile([P, I], F32, name="pd")
+        den = sb.tile([P, G], F32, name="den")
         num = sb.tile([P, G], F32, name="num")
         inv = sb.tile([P, G], F32, name="inv")
         res = sb.tile([P, G], F32, name="res")
 
-        def scores(c):
-            codes = sb.tile([P, CI], U32, name="xc%d" % c, align_bytes=64)
-            scales = sb.tile([P, CI], U8, name="xs%d" % c, align_bytes=64)
-            nc.vector.quantize_mx(out=codes[:].bitcast(FP8X4), scales=scales[:], in_=xw[c][:].rearrange("p i t -> p (i t)"))
+        def by_place(ap):
+            return ap.rearrange("p (g j) -> p g j", j=J)
+
+        def scores(q):
+            a, b = passes[q]
+            k = holder(banks, a)
+            codes = sb.tile([P, b - a], U32, name="xc%d" % q, align_bytes=64)
+            scales = sb.tile([P, b - a], U8, name="xs%d" % q, align_bytes=64)
+            nc.vector.quantize_mx(out=codes[:].bitcast(FP8X4), scales=scales[:], in_=xw[q][:].rearrange("p i t -> p (i t)"))
             nc.tensor.matmul_mx(
-                out=acc[c][:].rearrange("p g j -> p (g j)"),
+                out=acc[k][:, a - banks[k][0] : b - banks[k][0]],
                 lhsT=w_codes[:].bitcast(FP8X4),
                 lhsT_scale=w_scales[:],
                 rhs=codes[:].bitcast(FP8X4),
@@ -135,37 +168,65 @@ def tile_attend_costvolume_kernel(tc, fa, fb, wg, disp, offs, offs2, out):
                 stop=True,
             )
 
-        def largest(c):
-            nc.vector.tensor_reduce(top[c][:], acc[c][:], AX.X, ALU.max)
+        def largest(k):
+            a, b = banks[k]
+            nc.vector.tensor_reduce(top[:, a // J : b // J], by_place(acc[k][:]), AX.X, ALU.max)
 
-        def shift(c):
-            nc.vector.tensor_tensor(z[c][:], acc[c][:], top[c][:].unsqueeze(2).to_broadcast([P, CG, J]), ALU.subtract)
-            nc.scalar.activation(pr[c][:], z[c][:], ACT.Exp)
+        def shift(k):
+            a, b = banks[k]
+            wide = top[:, a // J : b // J].unsqueeze(2).to_broadcast([P, (b - a) // J, J])
+            nc.vector.tensor_tensor(by_place(z[:, a:b]), by_place(acc[k][:]), wide, ALU.subtract)
+            nc.scalar.activation(pr[:, a:b], z[:, a:b], ACT.Exp)
 
-        def weigh(c):
-            nc.vector.tensor_reduce(den[c][:], pr[c][:], AX.X, ALU.add)
-            eng = nc.vector if c == CHUNKS - 1 else nc.gpsimd
-            eng.tensor_tensor(pd[c][:].rearrange("p g j -> p (g j)"), pr[c][:].rearrange("p g j -> p (g j)"), d_flat[:, cols(c)], ALU.mult)
+        def by_scalar(k):
+            a, b = banks[k]
+            nc.vector.tensor_reduce(top[:, a // J : b // J], by_place(acc[k][:]), AX.X, ALU.max, negate=True)
 
-        def sums(c):
-            nc.vector.reciprocal(inv[:, c * CG : (c + 1) * CG], den[c][:])
-            nc.vector.tensor_reduce(num[:, c * CG : (c + 1) * CG], pd[c][:], AX.X, ALU.add)
+        def places(k):
+            a, b = banks[k]
+            for g in range(a // J, b // J):
+                nc.scalar.activation(pr[:, g * J : (g + 1) * J], acc[k][:, g * J - a : (g + 1) * J - a], ACT.Exp, bias=top[:, g : g + 1], accum_out=den[:, g : g + 1])
 
-        def finish(first, last):
-            span = slice(first * CG, (last + 1) * CG)
-            nc.vector.tensor_tensor(res[:, span], num[:, span], inv[:, span], ALU.mult)
+        def below(a, b):
+            nc.vector.tensor_reduce(den[:, a // J : b // J], by_place(pr[:, a:b]), AX.X, ALU.add)
 
-        for c in range(CHUNKS):
-            scores(c)
-        for c in range(CHUNKS):
-            largest(c)
-            shift(c)
-        last = CHUNKS - 1
-        weigh(last)
-        sums(last)
-        for c in range(last):
-            weigh(c)
-        for c in range(last):
-            sums(c)
-        finish(0, last)
+        def weigh(eng, a, b):
+            eng.tensor_tensor(pd[:, a:b], pr[:, a:b], d_flat[:, a:b], ALU.mult)
+
+        def invert(a, b):
+            nc.vector.reciprocal(inv[:, a // J : b // J], den[:, a // J : b // J])
+
+        def above(a, b):
+            nc.vector.tensor_reduce(num[:, a // J : b // J], by_place(pd[:, a:b]), AX.X, ALU.add)
+
+        for c in range(len(prods)):
+            product(3, c)
+            for k in range(len(weaves)):
+                if holder(prods, weaves[k][0]) == c:
+                    weave(k)
+            if prods[c][1] == HEAD:
+                ww = weights()
+        weights_rest(ww)
+        for q in range(len(passes)):
+            scores(q)
+        by_scalar(0)
+        places(0)
+        largest(1)
+        for k in range(2, len(banks)):
+            largest(k)
+            shift(k - 1)
+        shift(len(banks) - 1)
+        weigh(nc.vector, *banks[-1])
+        weigh(nc.vector, *banks[-2])
+        for a, b in banks[:-2]:
+            weigh(nc.gpsimd, a, b)
+        for a, b in banks[1:]:
+            below(a, b)
+        for a, b in banks:
+            invert(a, b)
+        for a, b in banks:
+            above(a, b)
+        cut = banks[-1][0] // J
+        nc.vector.tensor_tensor(res[:, 0:cut], num[:, 0:cut], inv[:, 0:cut], ALU.mult)
+        nc.vector.tensor_tensor(res[:, cut:G], num[:, cut:G], inv[:, cut:G], ALU.mult)
         nc.sync.dma_start(out, res[:])

@@ -17,34 +17,30 @@ P = 128
 PACK = 4
 D, T, I, G, M = 512, 1024, 512, 64, 128
 J = I // G
-PRODUCTS = [64, 128, 128, 64, 128]
-WEAVES = [(64, "s"), (128, "v"), (128, "v"), (64, "s"), (128, "s")]
-PASSES = [64, 128, 128, 64, 128]
-BANKS = [64, 128, 128, 64, 128]
+PER_COLUMN = 16
+
+SHORT, LONG = 64, 128
+WIDTHS = (SHORT, LONG, LONG, SHORT, LONG)
+WOVEN_BY_VECTOR = (1, 2)
+PIECES_ON_GPSIMD = 3
+HEAD_PIECES = 2
+GROUPS_ON_SCALAR = 96
 
 FLOPS = 2 * D * M * I
 
 
-def spans(widths):
-    out, at = [], 0
-    for w in widths:
-        out.append((at, at + w))
-        at = at + w
-    return out
-
-
-def holder(ranges, lo):
-    return [k for k, (a, b) in enumerate(ranges) if a <= lo < b][0]
-
-
 def tile_attend_costvolume_kernel(tc, fa, fb, wg, disp, offs, offs2, out):
     nc = tc.nc
+    pieces = [(sum(WIDTHS[:c]), sum(WIDTHS[: c + 1])) for c in range(len(WIDTHS))]
+    last = len(pieces) - 1
+    head = pieces[HEAD_PIECES][0]
+
     with ExitStack() as ctx:
         sb = ctx.enter_context(tc.tile_pool(name="sb", bufs=1))
         ps = ctx.enter_context(tc.psum_pool(name="ps", bufs=1))
 
-        list_a = sb.tile([P, I // 16], U16, name="list_a")
-        list_b = sb.tile([P, I // 16], U16, name="list_b")
+        list_a = sb.tile([P, I // PER_COLUMN], U16, name="list_a")
+        list_b = sb.tile([P, I // PER_COLUMN], U16, name="list_b")
         a_planes = [sb.tile([P, T], F32, name="a%d" % t) for t in range(PACK)]
         b_planes = [sb.tile([P, T], F32, name="b%d" % t) for t in range(PACK)]
         w_raw = sb.tile([P, PACK, M], F32, name="w_raw")
@@ -70,42 +66,30 @@ def tile_attend_costvolume_kernel(tc, fa, fb, wg, disp, offs, offs2, out):
         ident = sb.tile([P, P], F32, name="ident")
         make_identity(nc, ident[:])
 
-        prods = spans(PRODUCTS)
-        weaves = spans([w for w, e in WEAVES])
-        passes = spans(PASSES)
-        banks = spans(BANKS)
         b_got = [sb.tile([P, I], F32, name="bg%d" % t) for t in range(PACK - 1)]
-        HEAD = 192
-        b3_head = sb.tile([P, HEAD], F32, name="b3_head", tag="head", align_bytes=64)
-        b3_rest = sb.tile([P, I - HEAD], F32, name="b3_rest")
+        fb3_head = sb.tile([P, head], F32, name="b3_head", tag="head", align_bytes=64)
+        fb3_rest = sb.tile([P, I - head], F32, name="b3_rest")
         x01 = sb.tile([P, 2, I], F32, name="x01")
-        x23 = [sb.tile([P, 2, b - a], F32, name="x23_%d" % c) for c, (a, b) in enumerate(prods)]
-        xw = [sb.tile([P, b - a, PACK], BF16, name="xw%d" % c, align_bytes=64) for c, (a, b) in enumerate(passes)]
+        x23 = [sb.tile([P, 2, b - a], F32, name="x23_%d" % c) for c, (a, b) in enumerate(pieces)]
+        xw = [sb.tile([P, b - a, PACK], BF16, name="xw%d" % c, align_bytes=64) for c, (a, b) in enumerate(pieces)]
 
-        def gather_b(t):
-            nc.vector.tensor_copy(b_got[t][:], b_planes[t][:].indirect(list_b[:]))
+        def entries(list_tile, a, b):
+            return list_tile[:, a // PER_COLUMN : b // PER_COLUMN]
 
-        def product(t, c):
-            a, b = prods[c]
-            nc.vector.tensor_tensor(
-                x23[c][:, t - 2, :],
-                a_planes[t][:].indirect(list_a[:, a // 16 : b // 16]),
-                b_got[t][:, a:b] if t < 3 else (b3_head[:, a:b] if b <= HEAD else b3_rest[:, a - HEAD : b - HEAD]),
-                ALU.mult,
-            )
+        def gather_b(dst, t, a, b):
+            nc.vector.tensor_copy(dst, b_planes[t][:].indirect(entries(list_b, a, b)))
 
-        def weave(k):
-            a, b = weaves[k]
-            c, q = holder(prods, a), holder(passes, a)
-            dst = xw[q][:, a - passes[q][0] : b - passes[q][0], 2:4]
-            src = x23[c][:, :, a - prods[c][0] : b - prods[c][0]].rearrange("p t i -> p i t")
-            if WEAVES[k][1] == "v":
+        def product(dst, t, a, b, b_cols):
+            nc.vector.tensor_tensor(dst, a_planes[t][:].indirect(entries(list_a, a, b)), b_cols, ALU.mult)
+
+        def interleave(on_vector, dst, src):
+            if on_vector:
                 nc.vector.tensor_copy(dst, src)
             else:
                 nc.scalar.copy(dst, src)
 
-        gather_b(0)
-        nc.vector.tensor_tensor(x01[:, 0, :], a_planes[0][:].indirect(list_a[:]), b_got[0][:], ALU.mult)
+        gather_b(b_got[0][:], 0, 0, I)
+        product(x01[:, 0, :], 0, 0, I, b_got[0][:])
 
         d_turned = ps.tile([P, P], F32, name="d_turned")
         nc.tensor.transpose(d_turned[:], d_rows[:], ident[:])
@@ -113,33 +97,24 @@ def tile_attend_costvolume_kernel(tc, fa, fb, wg, disp, offs, offs2, out):
         d_ps = ps.tile([P, PACK, P], F32, name="d_ps")
         for q in range(PACK):
             nc.tensor.transpose(d_ps[:, q, :], d_cols[:, q : q + 1].to_broadcast([P, P]), ident[:])
-        d_all = sb.tile([P, PACK, P], F32, name="d_all")
-        nc.scalar.copy(d_all[:], d_ps[:])
-        d_flat = d_all[:].rearrange("p q n -> p (q n)")
+        d_psum = d_ps[:].rearrange("p q n -> p (q n)")
+        d_sbuf = sb.tile([P, pieces[PIECES_ON_GPSIMD][0]], F32, name="d_sbuf")
+        nc.scalar.copy(d_sbuf[:], d_psum[:, 0 : pieces[PIECES_ON_GPSIMD][0]])
 
         w_codes = sb.tile([P, M], U32, name="w_codes", align_bytes=64)
         w_scales = sb.tile([P, M], U8, name="w_scales", align_bytes=64)
 
-        def weights():
-            ww = sb.tile([P, M, PACK], BF16, name="ww", tag="head", align_bytes=64)
-            nc.scalar.copy(ww[:, 0:96, :], w_raw[:, :, 0:96].rearrange("p t m -> p m t"))
-            return ww
+        gather_b(b_got[1][:], 1, 0, I)
+        product(x01[:, 1, :], 1, 0, I, b_got[1][:])
+        for c, (a, b) in enumerate(pieces):
+            nc.scalar.copy(xw[c][:, :, 0:2], x01[:, :, a:b].rearrange("p t i -> p i t"))
+        gather_b(b_got[2][:], 2, 0, I)
+        gather_b(fb3_head[:], 3, 0, head)
+        gather_b(fb3_rest[:], 3, head, I)
+        for c, (a, b) in enumerate(pieces):
+            product(x23[c][:, 0, :], 2, a, b, b_got[2][:, a:b])
 
-        def weights_rest(ww):
-            nc.vector.tensor_copy(ww[:, 96:M, :], w_raw[:, :, 96:M].rearrange("p t m -> p m t"))
-            nc.vector.quantize_mx(out=w_codes[:].bitcast(FP8X4), scales=w_scales[:], in_=ww[:].rearrange("p m t -> p (m t)"))
-
-        gather_b(1)
-        nc.vector.tensor_tensor(x01[:, 1, :], a_planes[1][:].indirect(list_a[:]), b_got[1][:], ALU.mult)
-        for q, (a, b) in enumerate(passes):
-            nc.scalar.copy(xw[q][:, :, 0:2], x01[:, :, a:b].rearrange("p t i -> p i t"))
-        gather_b(2)
-        nc.vector.tensor_copy(b3_head[:], b_planes[3][:].indirect(list_b[:, 0 : HEAD // 16]))
-        nc.vector.tensor_copy(b3_rest[:], b_planes[3][:].indirect(list_b[:, HEAD // 16 : I // 16]))
-        for c in range(len(prods)):
-            product(2, c)
-
-        acc = [ps.tile([M, b - a], F32, name="acc%d" % c) for c, (a, b) in enumerate(banks)]
+        acc = [ps.tile([M, b - a], F32, name="acc%d" % c) for c, (a, b) in enumerate(pieces)]
         top = sb.tile([P, G], F32, name="top")
         z = sb.tile([P, I], F32, name="z")
         pr = sb.tile([P, I], F32, name="pr")
@@ -152,14 +127,25 @@ def tile_attend_costvolume_kernel(tc, fa, fb, wg, disp, offs, offs2, out):
         def by_place(ap):
             return ap.rearrange("p (g j) -> p g j", j=J)
 
-        def scores(q):
-            a, b = passes[q]
-            k = holder(banks, a)
-            codes = sb.tile([P, b - a], U32, name="xc%d" % q, align_bytes=64)
-            scales = sb.tile([P, b - a], U8, name="xs%d" % q, align_bytes=64)
-            nc.vector.quantize_mx(out=codes[:].bitcast(FP8X4), scales=scales[:], in_=xw[q][:].rearrange("p i t -> p (i t)"))
+        def pairs(c):
+            return slice(pieces[c][0], pieces[c][1])
+
+        def places(c):
+            return slice(pieces[c][0] // J, pieces[c][1] // J)
+
+        def last_plane(c, b_cols):
+            product(x23[c][:, 1, :], 3, pieces[c][0], pieces[c][1], b_cols)
+            interleave(c in WOVEN_BY_VECTOR, xw[c][:, :, 2:4], x23[c][:].rearrange("p t i -> p i t"))
+
+        def interleave_w(on_vector, dst, groups):
+            interleave(on_vector, dst[:, groups, :], w_raw[:, :, groups].rearrange("p t m -> p m t"))
+
+        def scores(c):
+            codes = sb.tile([P, WIDTHS[c]], U32, name="xc%d" % c, align_bytes=64)
+            scales = sb.tile([P, WIDTHS[c]], U8, name="xs%d" % c, align_bytes=64)
+            nc.vector.quantize_mx(out=codes[:].bitcast(FP8X4), scales=scales[:], in_=xw[c][:].rearrange("p i t -> p (i t)"))
             nc.tensor.matmul_mx(
-                out=acc[k][:, a - banks[k][0] : b - banks[k][0]],
+                out=acc[c][:],
                 lhsT=w_codes[:].bitcast(FP8X4),
                 lhsT_scale=w_scales[:],
                 rhs=codes[:].bitcast(FP8X4),
@@ -168,65 +154,48 @@ def tile_attend_costvolume_kernel(tc, fa, fb, wg, disp, offs, offs2, out):
                 stop=True,
             )
 
-        def largest(k):
-            a, b = banks[k]
-            nc.vector.tensor_reduce(top[:, a // J : b // J], by_place(acc[k][:]), AX.X, ALU.max)
+        def largest(c):
+            nc.vector.tensor_reduce(top[:, places(c)], by_place(acc[c][:]), AX.X, ALU.max)
 
-        def shift(k):
-            a, b = banks[k]
-            wide = top[:, a // J : b // J].unsqueeze(2).to_broadcast([P, (b - a) // J, J])
-            nc.vector.tensor_tensor(by_place(z[:, a:b]), by_place(acc[k][:]), wide, ALU.subtract)
-            nc.scalar.activation(pr[:, a:b], z[:, a:b], ACT.Exp)
+        def shift_and_exp(c):
+            wide = top[:, places(c)].unsqueeze(2).to_broadcast([P, WIDTHS[c] // J, J])
+            nc.vector.tensor_tensor(by_place(z[:, pairs(c)]), by_place(acc[c][:]), wide, ALU.subtract)
+            nc.scalar.activation(pr[:, pairs(c)], z[:, pairs(c)], ACT.Exp)
 
-        def by_scalar(k):
-            a, b = banks[k]
-            nc.vector.tensor_reduce(top[:, a // J : b // J], by_place(acc[k][:]), AX.X, ALU.max, negate=True)
+        def weigh(engine, c, d_wide):
+            engine.tensor_tensor(pd[:, pairs(c)], pr[:, pairs(c)], d_wide[:, pairs(c)], ALU.mult)
 
-        def places(k):
-            a, b = banks[k]
-            for g in range(a // J, b // J):
-                nc.scalar.activation(pr[:, g * J : (g + 1) * J], acc[k][:, g * J - a : (g + 1) * J - a], ACT.Exp, bias=top[:, g : g + 1], accum_out=den[:, g : g + 1])
+        for c in range(HEAD_PIECES):
+            last_plane(c, fb3_head[:, pairs(c)])
+        ww = sb.tile([P, M, PACK], BF16, name="ww", tag="head", align_bytes=64)
+        interleave_w(False, ww, slice(0, GROUPS_ON_SCALAR))
+        for c in range(HEAD_PIECES, len(pieces)):
+            last_plane(c, fb3_rest[:, pieces[c][0] - head : pieces[c][1] - head])
+        interleave_w(True, ww, slice(GROUPS_ON_SCALAR, M))
+        nc.vector.quantize_mx(out=w_codes[:].bitcast(FP8X4), scales=w_scales[:], in_=ww[:].rearrange("p m t -> p (m t)"))
+        for c in range(len(pieces)):
+            scores(c)
 
-        def below(a, b):
-            nc.vector.tensor_reduce(den[:, a // J : b // J], by_place(pr[:, a:b]), AX.X, ALU.add)
-
-        def weigh(eng, a, b):
-            eng.tensor_tensor(pd[:, a:b], pr[:, a:b], d_flat[:, a:b], ALU.mult)
-
-        def invert(a, b):
-            nc.vector.reciprocal(inv[:, a // J : b // J], den[:, a // J : b // J])
-
-        def above(a, b):
-            nc.vector.tensor_reduce(num[:, a // J : b // J], by_place(pd[:, a:b]), AX.X, ALU.add)
-
-        for c in range(len(prods)):
-            product(3, c)
-            for k in range(len(weaves)):
-                if holder(prods, weaves[k][0]) == c:
-                    weave(k)
-            if prods[c][1] == HEAD:
-                ww = weights()
-        weights_rest(ww)
-        for q in range(len(passes)):
-            scores(q)
-        by_scalar(0)
-        places(0)
+        nc.vector.tensor_reduce(top[:, places(0)], by_place(acc[0][:]), AX.X, ALU.max, negate=True)
+        for g in range(WIDTHS[0] // J):
+            own = slice(g * J, (g + 1) * J)
+            nc.scalar.activation(pr[:, own], acc[0][:, own], ACT.Exp, bias=top[:, g : g + 1], accum_out=den[:, g : g + 1])
         largest(1)
-        for k in range(2, len(banks)):
-            largest(k)
-            shift(k - 1)
-        shift(len(banks) - 1)
-        weigh(nc.vector, *banks[-1])
-        weigh(nc.vector, *banks[-2])
-        for a, b in banks[:-2]:
-            weigh(nc.gpsimd, a, b)
-        for a, b in banks[1:]:
-            below(a, b)
-        for a, b in banks:
-            invert(a, b)
-        for a, b in banks:
-            above(a, b)
-        cut = banks[-1][0] // J
-        nc.vector.tensor_tensor(res[:, 0:cut], num[:, 0:cut], inv[:, 0:cut], ALU.mult)
-        nc.vector.tensor_tensor(res[:, cut:G], num[:, cut:G], inv[:, cut:G], ALU.mult)
+        for c in range(2, len(pieces)):
+            largest(c)
+            shift_and_exp(c - 1)
+        shift_and_exp(last)
+
+        for c in range(last, PIECES_ON_GPSIMD - 1, -1):
+            weigh(nc.vector, c, d_psum)
+        for c in range(PIECES_ON_GPSIMD):
+            weigh(nc.gpsimd, c, d_sbuf)
+        for c in range(1, len(pieces)):
+            nc.vector.tensor_reduce(den[:, places(c)], by_place(pr[:, pairs(c)]), AX.X, ALU.add)
+        for c in range(len(pieces)):
+            nc.vector.reciprocal(inv[:, places(c)], den[:, places(c)])
+        for c in range(len(pieces)):
+            nc.vector.tensor_reduce(num[:, places(c)], by_place(pd[:, pairs(c)]), AX.X, ALU.add)
+        for part in (slice(0, pieces[last][0] // J), places(last)):
+            nc.vector.tensor_tensor(res[:, part], num[:, part], inv[:, part], ALU.mult)
         nc.sync.dma_start(out, res[:])

@@ -24,7 +24,7 @@ WIDTHS = (SHORT, LONG, LONG, SHORT, LONG)
 WOVEN_BY_VECTOR = (1, 2)
 PIECES_ON_GPSIMD = 3
 HEAD_PIECES = 2
-GROUPS_ON_SCALAR = 96
+GROUPS_ON_SCALAR = 64
 
 FLOPS = 2 * D * M * I
 
@@ -133,23 +133,25 @@ def tile_attend_costvolume_kernel(tc, fa, fb, wg, disp, offs, offs2, out):
         def places(c):
             return slice(pieces[c][0] // J, pieces[c][1] // J)
 
-        def last_plane(c, b_cols):
-            product(x23[c][:, 1, :], 3, pieces[c][0], pieces[c][1], b_cols)
+        def weave(c):
             interleave(c in WOVEN_BY_VECTOR, xw[c][:, :, 2:4], x23[c][:].rearrange("p t i -> p i t"))
 
         def interleave_w(on_vector, dst, groups):
             interleave(on_vector, dst[:, groups, :], w_raw[:, :, groups].rearrange("p t m -> p m t"))
 
+        codes = [sb.tile([P, w], U32, name="xc%d" % c, align_bytes=64) for c, w in enumerate(WIDTHS)]
+        scales = [sb.tile([P, w], U8, name="xs%d" % c, align_bytes=64) for c, w in enumerate(WIDTHS)]
+
+        def quantise(c):
+            nc.vector.quantize_mx(out=codes[c][:].bitcast(FP8X4), scales=scales[c][:], in_=xw[c][:].rearrange("p i t -> p (i t)"))
+
         def scores(c):
-            codes = sb.tile([P, WIDTHS[c]], U32, name="xc%d" % c, align_bytes=64)
-            scales = sb.tile([P, WIDTHS[c]], U8, name="xs%d" % c, align_bytes=64)
-            nc.vector.quantize_mx(out=codes[:].bitcast(FP8X4), scales=scales[:], in_=xw[c][:].rearrange("p i t -> p (i t)"))
             nc.tensor.matmul_mx(
                 out=acc[c][:],
                 lhsT=w_codes[:].bitcast(FP8X4),
                 lhsT_scale=w_scales[:],
-                rhs=codes[:].bitcast(FP8X4),
-                rhs_scale=scales[:],
+                rhs=codes[c][:].bitcast(FP8X4),
+                rhs_scale=scales[c][:],
                 start=True,
                 stop=True,
             )
@@ -165,15 +167,24 @@ def tile_attend_costvolume_kernel(tc, fa, fb, wg, disp, offs, offs2, out):
         def weigh(engine, c, d_wide):
             engine.tensor_tensor(pd[:, pairs(c)], pr[:, pairs(c)], d_wide[:, pairs(c)], ALU.mult)
 
-        for c in range(HEAD_PIECES):
-            last_plane(c, fb3_head[:, pairs(c)])
+        fb3 = [fb3_head[:, pairs(c)] if c < HEAD_PIECES else fb3_rest[:, pieces[c][0] - head : pieces[c][1] - head] for c in range(len(pieces))]
+        for c in range(len(pieces)):
+            product(x23[c][:, 1, :], 3, pieces[c][0], pieces[c][1], fb3[c])
+        weave(0)
         ww = sb.tile([P, M, PACK], BF16, name="ww", tag="head", align_bytes=64)
         interleave_w(False, ww, slice(0, GROUPS_ON_SCALAR))
-        for c in range(HEAD_PIECES, len(pieces)):
-            last_plane(c, fb3_rest[:, pieces[c][0] - head : pieces[c][1] - head])
         interleave_w(True, ww, slice(GROUPS_ON_SCALAR, M))
+        quantise(0)
+        weave(1)
         nc.vector.quantize_mx(out=w_codes[:].bitcast(FP8X4), scales=w_scales[:], in_=ww[:].rearrange("p m t -> p (m t)"))
-        for c in range(len(pieces)):
+        weave(3)
+        weave(4)
+        quantise(1)
+        weave(2)
+        quantise(3)
+        quantise(2)
+        quantise(4)
+        for c in (0, 1, 3, 2, 4):
             scores(c)
 
         nc.vector.tensor_reduce(top[:, places(0)], by_place(acc[0][:]), AX.X, ALU.max, negate=True)

@@ -22,9 +22,9 @@ PER_COLUMN = 16
 SHORT, LONG = 64, 128
 WIDTHS = (SHORT, LONG, LONG, SHORT, LONG)
 WOVEN_BY_VECTOR = (1, 2)
-PIECES_ON_GPSIMD = 3
+PIECES_ON_GPSIMD = len(WIDTHS) - 1
 HEAD_PIECES = 2
-GROUPS_ON_SCALAR = 64
+GROUPS_ON_SCALAR = M // 2
 
 FLOPS = 2 * D * M * I
 
@@ -167,9 +167,8 @@ def tile_attend_costvolume_kernel(tc, fa, fb, wg, disp, offs, offs2, out):
         def weigh(engine, c, d_wide):
             engine.tensor_tensor(pd[:, pairs(c)], pr[:, pairs(c)], d_wide[:, pairs(c)], ALU.mult)
 
-        fb3 = [fb3_head[:, pairs(c)] if c < HEAD_PIECES else fb3_rest[:, pieces[c][0] - head : pieces[c][1] - head] for c in range(len(pieces))]
-        for c in range(len(pieces)):
-            product(x23[c][:, 1, :], 3, pieces[c][0], pieces[c][1], fb3[c])
+        for c, (a, b) in enumerate(pieces):
+            product(x23[c][:, 1, :], 3, a, b, fb3_head[:, a:b] if c < HEAD_PIECES else fb3_rest[:, a - head : b - head])
         weave(0)
         ww = sb.tile([P, M, PACK], BF16, name="ww", tag="head", align_bytes=64)
         interleave_w(False, ww, slice(0, GROUPS_ON_SCALAR))
@@ -181,9 +180,8 @@ def tile_attend_costvolume_kernel(tc, fa, fb, wg, disp, offs, offs2, out):
         weave(4)
         quantise(1)
         weave(2)
-        quantise(3)
-        quantise(2)
-        quantise(4)
+        for c in (3, 2, 4):
+            quantise(c)
         for c in (0, 1, 3, 2, 4):
             scores(c)
 
@@ -197,16 +195,16 @@ def tile_attend_costvolume_kernel(tc, fa, fb, wg, disp, offs, offs2, out):
             shift_and_exp(c - 1)
         shift_and_exp(last)
 
-        for c in range(last, PIECES_ON_GPSIMD - 1, -1):
-            weigh(nc.vector, c, d_psum)
+        weigh(nc.vector, last, d_psum)
         for c in range(PIECES_ON_GPSIMD):
             weigh(nc.gpsimd, c, d_sbuf)
         for c in range(1, len(pieces)):
             nc.vector.tensor_reduce(den[:, places(c)], by_place(pr[:, pairs(c)]), AX.X, ALU.add)
-        for c in range(len(pieces)):
-            nc.vector.reciprocal(inv[:, places(c)], den[:, places(c)])
-        for c in range(len(pieces)):
+        late = slice(pieces[last - 1][0] // J, G)
+        for part in [places(c) for c in range(last - 1)] + [late]:
+            nc.vector.reciprocal(inv[:, part], den[:, part])
+        for c in list(range(last - 1)) + [last, last - 1]:
             nc.vector.tensor_reduce(num[:, places(c)], by_place(pd[:, pairs(c)]), AX.X, ALU.add)
-        for part in (slice(0, pieces[last][0] // J), places(last)):
+        for part in (slice(0, late.start), late):
             nc.vector.tensor_tensor(res[:, part], num[:, part], inv[:, part], ALU.mult)
         nc.sync.dma_start(out, res[:])

@@ -21,7 +21,7 @@ PER_COLUMN = 16
 
 SHORT, LONG = 64, 128
 WIDTHS = (SHORT, LONG, LONG, SHORT, LONG)
-WOVEN_BY_VECTOR = (1, 2)
+WOVEN_BY_VECTOR = (1, 4)
 PIECES_ON_GPSIMD = len(WIDTHS) - 1
 HEAD_PIECES = 2
 GROUPS_ON_SCALAR = M // 2
@@ -167,22 +167,23 @@ def tile_attend_costvolume_kernel(tc, fa, fb, wg, disp, offs, offs2, out):
         def weigh(engine, c, d_wide):
             engine.tensor_tensor(pd[:, pairs(c)], pr[:, pairs(c)], d_wide[:, pairs(c)], ALU.mult)
 
-        for c, (a, b) in enumerate(pieces):
+        for c in (0, 1, 4, 2, 3):
+            a, b = pieces[c]
             product(x23[c][:, 1, :], 3, a, b, fb3_head[:, a:b] if c < HEAD_PIECES else fb3_rest[:, a - head : b - head])
         weave(0)
         ww = sb.tile([P, M, PACK], BF16, name="ww", tag="head", align_bytes=64)
         interleave_w(False, ww, slice(0, GROUPS_ON_SCALAR))
         interleave_w(True, ww, slice(GROUPS_ON_SCALAR, M))
-        quantise(0)
         weave(1)
+        quantise(0)
         nc.vector.quantize_mx(out=w_codes[:].bitcast(FP8X4), scales=w_scales[:], in_=ww[:].rearrange("p m t -> p (m t)"))
-        weave(3)
-        weave(4)
-        quantise(1)
         weave(2)
-        for c in (3, 2, 4):
+        weave(3)
+        quantise(1)
+        weave(4)
+        for c in (2, 3, 4):
             quantise(c)
-        for c in (0, 1, 3, 2, 4):
+        for c in range(len(pieces)):
             scores(c)
 
         nc.vector.tensor_reduce(top[:, places(0)], by_place(acc[0][:]), AX.X, ALU.max, negate=True)

@@ -189,23 +189,31 @@ def tile_attend_costvolume_kernel(tc, fa, fb, wg, disp, offs, offs2, out):
         nc.vector.tensor_reduce(top[:, places(0)], by_place(acc[0][:]), AX.X, ALU.max, negate=True)
         for g in range(WIDTHS[0] // J):
             own = slice(g * J, (g + 1) * J)
-            nc.scalar.activation(pr[:, own], acc[0][:, own], ACT.Exp, bias=top[:, g : g + 1], accum_out=den[:, g : g + 1])
+            nc.scalar.activation(pr[:, own], acc[0][:, own], ACT.Exp, bias=top[:, g : g + 1])
         largest(1)
         for c in range(2, len(pieces)):
             largest(c)
             shift_and_exp(c - 1)
         shift_and_exp(last)
 
+        def span(first, final):
+            return slice(pieces[first][0], pieces[final][1]), slice(pieces[first][0] // J, pieces[final][1] // J)
+
+        def sums(dst, src, first, final):
+            cols, part = span(first, final)
+            nc.vector.tensor_reduce(dst[:, part], by_place(src[:, cols]), AX.X, ALU.add)
+
         weigh(nc.vector, last, d_psum)
         for c in range(PIECES_ON_GPSIMD):
             weigh(nc.gpsimd, c, d_sbuf)
-        for c in range(1, len(pieces)):
-            nc.vector.tensor_reduce(den[:, places(c)], by_place(pr[:, pairs(c)]), AX.X, ALU.add)
-        late = slice(pieces[last - 1][0] // J, G)
-        for part in [places(c) for c in range(last - 1)] + [late]:
+        for first, final in ((0, 0), (1, 1), (2, 2), (3, 3), (4, 4)):
+            sums(den, pr, first, final)
+        for first, final in ((0, 0), (1, 1), (2, 2), (3, 4)):
+            part = span(first, final)[1]
             nc.vector.reciprocal(inv[:, part], den[:, part])
-        for c in list(range(last - 1)) + [last, last - 1]:
-            nc.vector.tensor_reduce(num[:, places(c)], by_place(pd[:, pairs(c)]), AX.X, ALU.add)
-        for part in (slice(0, late.start), late):
+        for first, final in ((0, 0), (1, 1), (2, 2), (4, 4), (3, 3)):
+            sums(num, pd, first, final)
+        for first, final in ((0, 2), (3, 4)):
+            part = span(first, final)[1]
             nc.vector.tensor_tensor(res[:, part], num[:, part], inv[:, part], ALU.mult)
         nc.sync.dma_start(out, res[:])

@@ -116,8 +116,8 @@ def tile_attend_costvolume_kernel(tc, fa, fb, wg, disp, offs, offs2, out):
 
         acc = [ps.tile([M, b - a], F32, name="acc%d" % c) for c, (a, b) in enumerate(pieces)]
         top = sb.tile([P, G], F32, name="top")
-        z = sb.tile([P, I], F32, name="z")
-        pr = sb.tile([P, I], F32, name="pr")
+        z = {c: sb.tile([P, WIDTHS[c]], F32, name="z%d" % c, tag="z%d" % c) for c in (1, 2, 4)}
+        pr = {c: sb.tile([P, WIDTHS[c]], F32, name="pr%d" % c) for c in (0, 1, 2, 4)}
         pd = sb.tile([P, I], F32, name="pd")
         den = sb.tile([P, G], F32, name="den")
         num = sb.tile([P, G], F32, name="num")
@@ -161,11 +161,11 @@ def tile_attend_costvolume_kernel(tc, fa, fb, wg, disp, offs, offs2, out):
 
         def shift_and_exp(c):
             wide = top[:, places(c)].unsqueeze(2).to_broadcast([P, WIDTHS[c] // J, J])
-            nc.vector.tensor_tensor(by_place(z[:, pairs(c)]), by_place(acc[c][:]), wide, ALU.subtract)
-            nc.scalar.activation(pr[:, pairs(c)], z[:, pairs(c)], ACT.Exp)
+            nc.vector.tensor_tensor(by_place(z[c][:]), by_place(acc[c][:]), wide, ALU.subtract)
+            nc.scalar.activation(pr[c][:], z[c][:], ACT.Exp)
 
         def weigh(engine, c, d_wide):
-            engine.tensor_tensor(pd[:, pairs(c)], pr[:, pairs(c)], d_wide[:, pairs(c)], ALU.mult)
+            engine.tensor_tensor(pd[:, pairs(c)], pr[c][:], d_wide[:, pairs(c)], ALU.mult)
 
         for c in (0, 1, 4, 2, 3):
             a, b = pieces[c]
@@ -186,34 +186,38 @@ def tile_attend_costvolume_kernel(tc, fa, fb, wg, disp, offs, offs2, out):
         for c in range(len(pieces)):
             scores(c)
 
-        nc.vector.tensor_reduce(top[:, places(0)], by_place(acc[0][:]), AX.X, ALU.max, negate=True)
-        for g in range(WIDTHS[0] // J):
-            own = slice(g * J, (g + 1) * J)
-            nc.scalar.activation(pr[:, own], acc[0][:, own], ACT.Exp, bias=top[:, g : g + 1])
+        def largest_negated(c):
+            nc.vector.tensor_reduce(top[:, places(c)], by_place(acc[c][:]), AX.X, ALU.max, negate=True)
+
+        def exp_by_place(c):
+            for g in range(WIDTHS[c] // J):
+                place = pieces[c][0] // J + g
+                own = slice(g * J, (g + 1) * J)
+                total = den[:, place : place + 1] if c == 0 else None
+                nc.scalar.activation(pr[c][:, own], acc[c][:, own], ACT.Exp, bias=top[:, place : place + 1], accum_out=total)
+
+        largest_negated(0)
+        exp_by_place(0)
         largest(1)
-        for c in range(2, len(pieces)):
-            largest(c)
-            shift_and_exp(c - 1)
-        shift_and_exp(last)
-
-        def span(first, final):
-            return slice(pieces[first][0], pieces[final][1]), slice(pieces[first][0] // J, pieces[final][1] // J)
-
-        def sums(dst, src, first, final):
-            cols, part = span(first, final)
-            nc.vector.tensor_reduce(dst[:, part], by_place(src[:, cols]), AX.X, ALU.add)
+        largest(2)
+        shift_and_exp(1)
+        largest_negated(3)
+        largest(4)
+        shift_and_exp(2)
+        shift_and_exp(4)
+        pr[3] = sb.tile([P, WIDTHS[3]], F32, name="pr3", tag="z2")
+        exp_by_place(3)
 
         weigh(nc.vector, last, d_psum)
         for c in range(PIECES_ON_GPSIMD):
             weigh(nc.gpsimd, c, d_sbuf)
-        for first, final in ((0, 0), (1, 1), (2, 2), (3, 3), (4, 4)):
-            sums(den, pr, first, final)
-        for first, final in ((0, 0), (1, 1), (2, 2), (3, 4)):
-            part = span(first, final)[1]
-            nc.vector.reciprocal(inv[:, part], den[:, part])
-        for first, final in ((0, 0), (1, 1), (2, 2), (4, 4), (3, 3)):
-            sums(num, pd, first, final)
-        for first, final in ((0, 2), (3, 4)):
-            part = span(first, final)[1]
+        for c in (1, 2, 4, 3):
+            nc.vector.tensor_reduce(den[:, places(c)], by_place(pr[c][:]), AX.X, ALU.add)
+        for c in (0, 1, 2, 4, 3):
+            nc.vector.reciprocal(inv[:, places(c)], den[:, places(c)])
+        for c in (0, 1, 2, 4, 3):
+            nc.vector.tensor_reduce(num[:, places(c)], by_place(pd[:, pairs(c)]), AX.X, ALU.add)
+        late = places(3).start
+        for part in (slice(0, late), slice(late, G)):
             nc.vector.tensor_tensor(res[:, part], num[:, part], inv[:, part], ALU.mult)
         nc.sync.dma_start(out, res[:])

@@ -115,7 +115,7 @@ def tile_attend_costvolume_kernel(tc, fa, fb, wg, disp, offs, offs2, out):
             product(x23[c][:, 0, :], 2, a, b, b_got[2][:, a:b])
 
         acc = [ps.tile([M, b - a], F32, name="acc%d" % c) for c, (a, b) in enumerate(pieces)]
-        top = sb.tile([P, G], F32, name="top")
+        top = {c: sb.tile([P, WIDTHS[c] // J], F32, name="top%d" % c, tag="top%d" % c) for c in (0, 1, 2, 4)}
         z = {c: sb.tile([P, WIDTHS[c]], F32, name="z%d" % c, tag="z%d" % c) for c in (1, 2, 4)}
         pr = {c: sb.tile([P, WIDTHS[c]], F32, name="pr%d" % c) for c in (0, 1, 2, 4)}
         pd = sb.tile([P, I], F32, name="pd")
@@ -157,10 +157,10 @@ def tile_attend_costvolume_kernel(tc, fa, fb, wg, disp, offs, offs2, out):
             )
 
         def largest(c):
-            nc.vector.tensor_reduce(top[:, places(c)], by_place(acc[c][:]), AX.X, ALU.max)
+            nc.vector.tensor_reduce(top[c][:], by_place(acc[c][:]), AX.X, ALU.max)
 
         def shift_and_exp(c):
-            wide = top[:, places(c)].unsqueeze(2).to_broadcast([P, WIDTHS[c] // J, J])
+            wide = top[c][:].unsqueeze(2).to_broadcast([P, WIDTHS[c] // J, J])
             nc.vector.tensor_tensor(by_place(z[c][:]), by_place(acc[c][:]), wide, ALU.subtract)
             nc.scalar.activation(pr[c][:], z[c][:], ACT.Exp)
 
@@ -187,23 +187,24 @@ def tile_attend_costvolume_kernel(tc, fa, fb, wg, disp, offs, offs2, out):
             scores(c)
 
         def largest_negated(c):
-            nc.vector.tensor_reduce(top[:, places(c)], by_place(acc[c][:]), AX.X, ALU.max, negate=True)
+            nc.vector.tensor_reduce(top[c][:], by_place(acc[c][:]), AX.X, ALU.max, negate=True)
 
         def exp_by_place(c):
             for g in range(WIDTHS[c] // J):
                 place = pieces[c][0] // J + g
                 own = slice(g * J, (g + 1) * J)
                 total = den[:, place : place + 1] if c == 0 else None
-                nc.scalar.activation(pr[c][:, own], acc[c][:, own], ACT.Exp, bias=top[:, place : place + 1], accum_out=total)
+                nc.scalar.activation(pr[c][:, own], acc[c][:, own], ACT.Exp, bias=top[c][:, g : g + 1], accum_out=total)
 
         largest_negated(0)
         exp_by_place(0)
         largest(1)
         largest(2)
         shift_and_exp(1)
-        largest_negated(3)
         largest(4)
         shift_and_exp(2)
+        top[3] = sb.tile([P, WIDTHS[3] // J], F32, name="top3", tag="top1")
+        largest_negated(3)
         shift_and_exp(4)
         pr[3] = sb.tile([P, WIDTHS[3]], F32, name="pr3", tag="z2")
         exp_by_place(3)

@@ -191,10 +191,8 @@ def tile_attend_costvolume_kernel(tc, fa, fb, wg, disp, offs, offs2, out):
 
         def exp_by_place(c):
             for g in range(WIDTHS[c] // J):
-                place = pieces[c][0] // J + g
                 own = slice(g * J, (g + 1) * J)
-                total = den[:, place : place + 1] if c == 0 else None
-                nc.scalar.activation(pr[c][:, own], acc[c][:, own], ACT.Exp, bias=top[c][:, g : g + 1], accum_out=total)
+                nc.scalar.activation(pr[c][:, own], acc[c][:, own], ACT.Exp, bias=top[c][:, g : g + 1])
 
         largest_negated(0)
         exp_by_place(0)
@@ -212,7 +210,7 @@ def tile_attend_costvolume_kernel(tc, fa, fb, wg, disp, offs, offs2, out):
         weigh(nc.vector, last, d_psum)
         for c in range(PIECES_ON_GPSIMD):
             weigh(nc.gpsimd, c, d_sbuf)
-        for c in (1, 2, 4, 3):
+        for c in (0, 1, 2, 4, 3):
             nc.vector.tensor_reduce(den[:, places(c)], by_place(pr[c][:]), AX.X, ALU.add)
         for c in (0, 1, 2, 4, 3):
             nc.vector.reciprocal(inv[:, places(c)], den[:, places(c)])

from contextlib import ExitStack

import concourse.mybir as mybir
from concourse.masks import make_identity

F32 = mybir.dt.float32
BF16 = mybir.dt.bfloat16
U32 = mybir.dt.uint32
U16 = mybir.dt.uint16
U8 = mybir.dt.uint8
FP8X4 = mybir.dt.float8_e4m3fn_x4
ALU = mybir.AluOpType
ACT = mybir.ActivationFunctionType
AX = mybir.AxisListType

P = 128
PACK = 4
D, T, I, G, M = 512, 1024, 512, 64, 128
J = I // G
PER_COLUMN = 16

SHORT, LONG = 64, 128
WIDTHS = (SHORT, LONG, LONG, SHORT, LONG)
WOVEN_BY_VECTOR = (1, 4)
PIECES_ON_GPSIMD = len(WIDTHS) - 1
HEAD_PIECES = 2
GROUPS_ON_SCALAR = M // 2

FLOPS = 2 * D * M * I


def tile_attend_costvolume_kernel(tc, fa, fb, wg, disp, offs, offs2, out):
    nc = tc.nc
    pieces = [(sum(WIDTHS[:c]), sum(WIDTHS[: c + 1])) for c in range(len(WIDTHS))]
    last = len(pieces) - 1
    head = pieces[HEAD_PIECES][0]

    with ExitStack() as ctx:
        sb = ctx.enter_context(tc.tile_pool(name="sb", bufs=1))
        ps = ctx.enter_context(tc.psum_pool(name="ps", bufs=1))

        list_a = sb.tile([P, I // PER_COLUMN], U16, name="list_a")
        list_b = sb.tile([P, I // PER_COLUMN], U16, name="list_b")
        a_planes = [sb.tile([P, T], F32, name="a%d" % t) for t in range(PACK)]
        b_planes = [sb.tile([P, T], F32, name="b%d" % t) for t in range(PACK)]
        w_raw = sb.tile([P, PACK, M], F32, name="w_raw")
        d_cols = sb.tile([P, PACK], F32, name="d_cols")
        d_rows = sb.tile([P, P], F32, name="d_rows")
        fa_v = fa.rearrange("(p t) c -> p t c", t=PACK)
        fb_v = fb.rearrange("(p t) c -> p t c", t=PACK)

        nc.sync.dma_start(b_planes[0][:], fb_v[:, 0, :])
        nc.sync.dma_start(list_b[:], offs2)
        nc.sync.dma_start(list_a[:], offs)
        nc.sync.dma_start(a_planes[0][:], fa_v[:, 0, :])
        nc.gpsimd.memset(d_rows[:], 0.0)
        nc.scalar.dma_start(d_rows[0:PACK, :], disp.rearrange("o (q n) -> (o q) n", q=PACK))
        nc.sync.dma_start(b_planes[1][:], fb_v[:, 1, :])
        nc.sync.dma_start(a_planes[1][:], fa_v[:, 1, :])
        nc.sync.dma_start(b_planes[2][:], fb_v[:, 2, :])
        nc.sync.dma_start(b_planes[3][:], fb_v[:, 3, :])
        nc.sync.dma_start(a_planes[2][:], fa_v[:, 2, :])
        nc.sync.dma_start(a_planes[3][:], fa_v[:, 3, :])
        nc.sync.dma_start(w_raw[:], wg.rearrange("(p t) m -> p t m", t=PACK))

        ident = sb.tile([P, P], F32, name="ident")
        make_identity(nc, ident[:])

        b_got = [sb.tile([P, I], F32, name="bg%d" % t) for t in range(PACK - 1)]
        fb3_head = sb.tile([P, head], F32, name="b3_head", tag="head", align_bytes=64)
        fb3_rest = sb.tile([P, I - head], F32, name="b3_rest")
        x01 = sb.tile([P, 2, I], F32, name="x01")
        x23 = [sb.tile([P, 2, b - a], F32, name="x23_%d" % c) for c, (a, b) in enumerate(pieces)]
        xw = [sb.tile([P, b - a, PACK], BF16, name="xw%d" % c, align_bytes=64) for c, (a, b) in enumerate(pieces)]

        def entries(list_tile, a, b):
            return list_tile[:, a // PER_COLUMN : b // PER_COLUMN]

        def gather_b(dst, t, a, b):
            nc.vector.tensor_copy(dst, b_planes[t][:].indirect(entries(list_b, a, b)))

        def product(dst, t, a, b, b_cols):
            nc.vector.tensor_tensor(dst, a_planes[t][:].indirect(entries(list_a, a, b)), b_cols, ALU.mult)

        def interleave(on_vector, dst, src):
            if on_vector:
                nc.vector.tensor_copy(dst, src)
            else:
                nc.scalar.copy(dst, src)

        gather_b(b_got[0][:], 0, 0, I)
        product(x01[:, 0, :], 0, 0, I, b_got[0][:])

        d_turned = ps.tile([P, P], F32, name="d_turned")
        nc.tensor.transpose(d_turned[:], d_rows[:], ident[:])
        nc.scalar.copy(d_cols[:], d_turned[:, 0:PACK])
        d_ps = ps.tile([P, PACK, P], F32, name="d_ps")
        for q in range(PACK):
            nc.tensor.transpose(d_ps[:, q, :], d_cols[:, q : q + 1].to_broadcast([P, P]), ident[:])
        d_psum = d_ps[:].rearrange("p q n -> p (q n)")
        d_sbuf = sb.tile([P, pieces[PIECES_ON_GPSIMD][0]], F32, name="d_sbuf")
        nc.scalar.copy(d_sbuf[:], d_psum[:, 0 : pieces[PIECES_ON_GPSIMD][0]])

        w_codes = sb.tile([P, M], U32, name="w_codes", align_bytes=64)
        w_scales = sb.tile([P, M], U8, name="w_scales", align_bytes=64)

        gather_b(b_got[1][:], 1, 0, I)
        product(x01[:, 1, :], 1, 0, I, b_got[1][:])
        for c, (a, b) in enumerate(pieces):
            nc.scalar.copy(xw[c][:, :, 0:2], x01[:, :, a:b].rearrange("p t i -> p i t"))
        gather_b(b_got[2][:], 2, 0, I)
        gather_b(fb3_head[:], 3, 0, head)
        gather_b(fb3_rest[:], 3, head, I)
        for c, (a, b) in enumerate(pieces):
            product(x23[c][:, 0, :], 2, a, b, b_got[2][:, a:b])

        acc = [ps.tile([M, b - a], F32, name="acc%d" % c) for c, (a, b) in enumerate(pieces)]
        top = {c: sb.tile([P, WIDTHS[c] // J], F32, name="top%d" % c, tag="top%d" % c) for c in (0, 1, 2, 4)}
        z = {c: sb.tile([P, WIDTHS[c]], F32, name="z%d" % c, tag="z%d" % c) for c in (1, 2, 4)}
        pr = {c: sb.tile([P, WIDTHS[c]], F32, name="pr%d" % c) for c in (0, 1, 2, 4)}
        pd = sb.tile([P, I], F32, name="pd")
        den = sb.tile([P, G], F32, name="den")
        num = sb.tile([P, G], F32, name="num")
        inv = sb.tile([P, G], F32, name="inv")
        res = sb.tile([P, G], F32, name="res")

        def by_place(ap):
            return ap.rearrange("p (g j) -> p g j", j=J)

        def pairs(c):
            return slice(pieces[c][0], pieces[c][1])

        def places(c):
            return slice(pieces[c][0] // J, pieces[c][1] // J)

        def weave(c):
            interleave(c in WOVEN_BY_VECTOR, xw[c][:, :, 2:4], x23[c][:].rearrange("p t i -> p i t"))

        def interleave_w(on_vector, dst, groups):
            interleave(on_vector, dst[:, groups, :], w_raw[:, :, groups].rearrange("p t m -> p m t"))

        codes = [sb.tile([P, w], U32, name="xc%d" % c, align_bytes=64) for c, w in enumerate(WIDTHS)]
        scales = [sb.tile([P, w], U8, name="xs%d" % c, align_bytes=64) for c, w in enumerate(WIDTHS)]

        def quantise(c):
            nc.vector.quantize_mx(out=codes[c][:].bitcast(FP8X4), scales=scales[c][:], in_=xw[c][:].rearrange("p i t -> p (i t)"))

        def scores(c):
            nc.tensor.matmul_mx(
                out=acc[c][:],
                lhsT=w_codes[:].bitcast(FP8X4),
                lhsT_scale=w_scales[:],
                rhs=codes[c][:].bitcast(FP8X4),
                rhs_scale=scales[c][:],
                start=True,
                stop=True,
            )

        def largest(c):
            nc.vector.tensor_reduce(top[c][:], by_place(acc[c][:]), AX.X, ALU.max)

        def shift_and_exp(c):
            wide = top[c][:].unsqueeze(2).to_broadcast([P, WIDTHS[c] // J, J])
            nc.vector.tensor_tensor(by_place(z[c][:]), by_place(acc[c][:]), wide, ALU.subtract)
            nc.scalar.activation(pr[c][:], z[c][:], ACT.Exp)

        def weigh(engine, c, d_wide):
            engine.tensor_tensor(pd[:, pairs(c)], pr[c][:], d_wide[:, pairs(c)], ALU.mult)

        for c in (0, 1, 4, 2, 3):
            a, b = pieces[c]
            product(x23[c][:, 1, :], 3, a, b, fb3_head[:, a:b] if c < HEAD_PIECES else fb3_rest[:, a - head : b - head])
        weave(0)
        ww = sb.tile([P, M, PACK], BF16, name="ww", tag="head", align_bytes=64)
        interleave_w(False, ww, slice(0, GROUPS_ON_SCALAR))
        interleave_w(True, ww, slice(GROUPS_ON_SCALAR, M))
        weave(1)
        quantise(0)
        nc.vector.quantize_mx(out=w_codes[:].bitcast(FP8X4), scales=w_scales[:], in_=ww[:].rearrange("p m t -> p (m t)"))
        weave(2)
        weave(3)
        quantise(1)
        weave(4)
        for c in (2, 3, 4):
            quantise(c)
        for c in range(len(pieces)):
            scores(c)

        def largest_negated(c):
            nc.vector.tensor_reduce(top[c][:], by_place(acc[c][:]), AX.X, ALU.max, negate=True)

        def exp_by_place(c):
            for g in range(WIDTHS[c] // J):
                own = slice(g * J, (g + 1) * J)
                nc.scalar.activation(pr[c][:, own], acc[c][:, own], ACT.Exp, bias=top[c][:, g : g + 1])

        largest_negated(0)
        exp_by_place(0)
        largest(1)
        largest(2)
        shift_and_exp(1)
        largest(4)
        shift_and_exp(2)
        top[3] = sb.tile([P, WIDTHS[3] // J], F32, name="top3", tag="top1")
        largest_negated(3)
        shift_and_exp(4)
        pr[3] = sb.tile([P, WIDTHS[3]], F32, name="pr3", tag="z2")
        exp_by_place(3)

        weigh(nc.vector, last, d_psum)
        for c in range(PIECES_ON_GPSIMD):
            weigh(nc.gpsimd, c, d_sbuf)
        for c in (0, 1, 2, 4, 3):
            nc.vector.tensor_reduce(den[:, places(c)], by_place(pr[c][:]), AX.X, ALU.add)
        for c in (0, 1, 2, 4, 3):
            nc.vector.reciprocal(inv[:, places(c)], den[:, places(c)])
        for c in (0, 1, 2, 4, 3):
            nc.vector.tensor_reduce(num[:, places(c)], by_place(pd[:, pairs(c)]), AX.X, ALU.add)
        late = places(3).start
        for part in (slice(0, late), slice(late, G)):
            nc.vector.tensor_tensor(res[:, part], num[:, part], inv[:, part], ALU.mult)
        nc.sync.dma_start(out, res[:])
